import numpy as np
import ml_dtypes


def mxq(x, axis, fmt="e4m3"):
    dtype, down = {"e4m3": (ml_dtypes.float8_e4m3fn, 7), "e5m2": (ml_dtypes.float8_e5m2, 14)}[fmt]
    v = np.moveaxis(np.asarray(x, np.float32).astype(ml_dtypes.bfloat16).astype(np.float64), axis, -1)
    blocks = v.reshape(v.shape[:-1] + (-1, 32))
    amax = np.abs(blocks).max(-1, keepdims=True)
    byte = np.maximum(np.where(amax > 0, np.frexp(amax)[1] - 1 + 127, 0) - down, 1)
    scale = np.exp2(byte - 127.0)
    codes = (blocks / scale).astype(np.float32).astype(dtype).astype(np.float64)
    return np.moveaxis((codes * scale).reshape(v.shape), -1, axis)


WIDE = False


def mx_kscale(k):
    if not WIDE:
        return np.ones(k)
    levels = np.array([10, -10, 5, -5, 0])
    if k % 512:
        return np.exp2(np.random.permutation(np.resize(levels, k // 32))).repeat(32)
    a = np.empty((k // 512, 16))
    for p in range(k // 512):
        a[p, :8] = np.random.permutation(np.resize(levels, 8))
        for g in range(8):
            far = levels[np.abs(levels - a[p, g]) >= 10]
            a[p, g + 8] = far[np.random.randint(len(far))]
    return np.exp2(a.ravel()).repeat(32)


def f64(x):
    return np.asarray(x).astype(np.float64)


def striped(idx):
    return np.tile(idx.reshape(-1, 16).T, (8, 1)).astype(np.uint16)


def unstriped(offs):
    return offs[:16].T.reshape(-1).astype(np.int64)


E2M1 = np.array([0.0, 0.5, 1.0, 1.5, 2.0, 3.0, 4.0, 6.0, -0.0, -0.5, -1.0, -1.5, -2.0, -3.0, -4.0, -6.0])


def pack_weight(w, fmt):
    k, n = w.shape
    w = f64(np.asarray(w, np.float32).astype(ml_dtypes.bfloat16)).reshape(k // 32, 32, n)
    amax = np.abs(w).max(1)
    if fmt == "e4m3":
        byte = np.frexp(amax)[1] - 1 + 127 - 7
    else:
        mant, ex = np.frexp(amax / 6.0)
        byte = np.where(mant > 0.5, ex, ex - 1) + 127
    byte = np.clip(np.where(amax > 0, byte, 1), 1, 254)
    scaled = (w * np.exp2(127.0 - byte)[:, None, :]).reshape(k, n).astype(np.float32)
    by_word = np.ascontiguousarray(scaled.reshape(k // 512, 128, 4, n).transpose(0, 1, 3, 2))
    if fmt == "e4m3":
        words = by_word.astype(ml_dtypes.float8_e4m3fn).view(np.uint8)
    else:
        c = by_word.astype(ml_dtypes.float4_e2m1fn).view(np.uint8) & 0xF
        words = (c[..., 0::2] | (c[..., 1::2] << 4)).reshape(k // 512, 128, 2 * n)
    return np.ascontiguousarray(words), np.ascontiguousarray(byte.astype(np.uint8).reshape(k // 512, 16, n))


def unpack_weight(words, scales, fmt):
    g, _, n = scales.shape
    words = np.ascontiguousarray(words).reshape(g, 128, n, -1)
    if fmt == "e4m3":
        vals = words.view(ml_dtypes.float8_e4m3fn).astype(np.float64)
    else:
        nib = np.empty((g, 128, n, 4), np.uint8)
        nib[..., 0::2] = words & 0xF
        nib[..., 1::2] = words >> 4
        vals = E2M1[nib]
    vals = vals * np.repeat(np.exp2(scales.astype(np.float64) - 127.0), 8, axis=1)[..., None]
    return vals.transpose(0, 1, 3, 2).reshape(g * 512, n)


def gelu(v):
    return 0.5 * v * (1.0 + np.tanh(np.sqrt(2.0 / np.pi) * (v + 0.044715 * v**3)))


K, T, E, C, N = 512, 1280, 15, 256, 256
TOP = 3


def by_expert(wq, xq):
    return np.concatenate([wq[e].T @ xq[:, e * C:(e + 1) * C] for e in range(E)], axis=1)


def setup_inputs():
    n = np.random.standard_normal
    s = mx_kscale(K)[:, None]
    deal = np.repeat(np.arange(E), C).reshape(TOP, T)[:, np.random.permutation(T)]
    deal = np.take_along_axis(deal, np.argsort(np.random.rand(TOP, T), axis=0), axis=0)
    for _ in range(8):
        s_, t_ = np.random.permutation(T).reshape(2, -1); r = np.random.randint(TOP, size=T // 2); x, y = deal[r, s_].copy(), deal[r, t_].copy()
        ok = ~((deal[:, s_] == y).any(0) | (deal[:, t_] == x).any(0)); deal[r[ok], s_[ok]] = y[ok]; deal[r[ok], t_[ok]] = x[ok]
    order = np.lexsort((np.random.rand(TOP * T), deal.reshape(-1)))
    slot_token = order % T; pos = np.empty(TOP * T, np.int64); pos[order] = np.arange(TOP * T); pos = pos.reshape(TOP, T)
    g = np.random.uniform(0.5, 1.5, (TOP, T)); g = g / g.sum(0)
    w = [pack_weight(m, "e2m1") for m in n((E + 1, K, N)) / np.sqrt(K) / s[None]]
    return {
        "xT": (n((K, T)) * s).astype(np.float32),
        "w_words": np.stack([m[0] for m in w]),
        "w_scales": np.stack([m[1] for m in w]),
        "b": (0.3 * n((N, E + 1))).astype(np.float32),
        "gate": np.stack([np.tile(r, (N, 1)) for r in g]).astype(np.float32),
        "offs": striped(slot_token),
        "pos1": striped(pos[0]),
        "pos2": striped(pos[1]),
        "pos3": striped(pos[2]),
    }


def reference(xT, w_words, w_scales, b, gate, offs, pos1, pos2, pos3):
    idx = unstriped(offs)
    w = np.stack([unpack_weight(w_words[e], w_scales[e], "e2m1") for e in range(E + 1)])
    wq = w
    xs = mxq(f64(xT), 0, "e4m3")
    ys = gelu((wq[E].T @ xs) + f64(b)[:, E:])
    xq = mxq(f64(xT)[:, idx], 0, "e4m3")
    y = by_expert(w, xq)
    y = gelu(y + np.repeat(f64(b)[:, :E], C, axis=1))
    return ys + sum(f64(gate[r]) * y[:, unstriped(p)] for r, p in enumerate((pos1, pos2, pos3)))

@@ -1,0 +1,196 @@
+from contextlib import ExitStack
+
+import concourse.mybir as mybir
+from concourse.masks import make_identity
+
+K, T, E, C, N = 512, 1280, 15, 256, 256
+TOP = 3
+SLOTS = E * C
+FLOPS = 2 * K * N * (SLOTS + T)
+
+F32 = mybir.dt.float32
+BF16 = mybir.dt.bfloat16
+I32 = mybir.dt.int32
+U32 = mybir.dt.uint32
+U16 = mybir.dt.uint16
+U8 = mybir.dt.uint8
+FP8X4 = mybir.dt.float8_e4m3fn_x4
+FP4X4 = mybir.dt.float4_e2m1fn_x4
+GELU = mybir.ActivationFunctionType.Gelu_apprx_tanh
+MULT = mybir.AluOpType.mult
+
+P = 128
+PACK = 4
+HALVES = N // P
+LIST_ROWS = 16
+BANK = 512
+
+
+def spans(widths):
+    out, at = [], 0
+    for w in widths:
+        out.append((at, at + w))
+        at += w
+    return out
+
+
+X_CHUNKS = spans([512, 512, 256])
+SLOT_GROUPS = spans([512] * 7 + [256])
+SHARED_GROUPS = spans([512, 512, 256])
+PIECES = spans([512, 512, 256])
+
+
+def tile_moe_shr_lin_gelu_kernel(tc, xT, w_words, w_scales, b, gate, offs, pos1, pos2, pos3, out):
+    nc = tc.nc
+    with ExitStack() as ctx:
+        keep = ctx.enter_context(tc.tile_pool(name="keep", bufs=1))
+        ring = ctx.enter_context(tc.tile_pool(name="ring", bufs=3))
+        stage = ctx.enter_context(tc.tile_pool(name="stage", bufs=6))
+        psum_mm = ctx.enter_context(tc.psum_pool(name="psum_mm", bufs=4))
+        psum_t = ctx.enter_context(tc.psum_pool(name="psum_t", bufs=2))
+
+        offs_sb = keep.tile([P, SLOTS // LIST_ROWS], U16, name="offs_sb")
+        nc.sync.dma_start(offs_sb[:], offs)
+
+        x_rows = xT.rearrange("(p j) t -> p j t", j=PACK)
+        raw = {}
+        for u in range(2):
+            for c0, c1 in X_CHUNKS:
+                raw[u, c0] = stage.tile([P, 2, c1 - c0], F32, name="staged")
+                nc.sync.dma_start(raw[u, c0][:], x_rows[:, 2 * u : 2 * u + 2, c0:c1])
+
+        w_plane = keep.tile([P, E + 1, N], U8, name="w_plane", align_bytes=64)
+        nc.vector.memset(w_plane[:].rearrange("p e n -> p (e n)").bitcast(I32), 0)
+        scale_rows = w_scales.rearrange("e a q n -> (a q) e n")
+        for quad in range(4):
+            nc.sync.dma_start(w_plane[32 * quad : 32 * quad + 4, :, :].bitcast(I32), scale_rows[4 * quad : 4 * quad + 4, :, :].bitcast(I32))
+        bias = keep.tile([P, HALVES, E + 1], F32, name="bias")
+        nc.sync.dma_start(bias[:], b.rearrange("(h p) e -> p h e", p=P))
+        w_sb = keep.tile([P, E + 1, 2 * N], U8, name="w_sb", align_bytes=64)
+        word_rows = w_words.rearrange("e a p n -> p (e a) n")
+        for e0 in (0, 8):
+            nc.sync.dma_start(w_sb[:, e0 : e0 + 8, :].bitcast(I32), word_rows[:, e0 : e0 + 8, :].bitcast(I32))
+        pos_sb = []
+        for r, pos in enumerate((pos1, pos2, pos3)):
+            tile = keep.tile([P, T // LIST_ROWS], U16, name=f"pos_sb{r}")
+            nc.sync.dma_start(tile[:], pos)
+            pos_sb.append(tile)
+
+        ident = keep.tile([P, P], F32, name="ident")
+        make_identity(nc, ident[:])
+
+        both = keep.tile([P, 2, 2 * T], BF16, name="both")
+        pairs = [both[:, u, :] for u in range(2)]
+        def cast(copy, u, c0, t0, t1):
+            copy(pairs[u][:, 2 * t0 : 2 * t1].rearrange("p (t e) -> p t e", e=2), raw[u, c0][:, :, t0 - c0 : t1 - c0].rearrange("p e t -> p t e"))
+
+        for c0, c1 in X_CHUNKS:
+            cut = c0 + 5 * (c1 - c0) // 8
+            cast(nc.vector.tensor_copy, 0, c0, c0, cut)
+            cast(nc.scalar.copy, 0, c0, cut, c1)
+        for c0, c1 in X_CHUNKS:
+            cast(nc.scalar.copy, 1, c0, c0, c1)
+
+        gate_sb = {}
+        for h in range(HALVES):
+            for r in range(TOP):
+                gate_sb[h, r] = stage.tile([P, T], F32, name="staged")
+                nc.sync.dma_start(gate_sb[h, r][:], gate[r, h * P : (h + 1) * P, :])
+
+        y = [keep.tile([P, SLOTS], F32, name=f"y{h}") for h in range(HALVES)]
+        ys = [keep.tile([P, T], F32, name=f"ys{h}") for h in range(HALVES)]
+
+        picked, grouped, codes, scales = {}, {}, {}, {}
+
+        def gather(g, u):
+            s0, s1 = SLOT_GROUPS[g]
+            if u == 0:
+                picked[g] = ring.tile([P, 2, 2 * (s1 - s0)], BF16, name="picked")
+            nc.vector.tensor_copy(picked[g][:, u, :].bitcast(U32), pairs[u].bitcast(U32).indirect(offs_sb[:, s0 // LIST_ROWS : s1 // LIST_ROWS]))
+
+        def interleave(g):
+            s0, s1 = SLOT_GROUPS[g]
+            grouped[g] = ring.tile([P, PACK * (s1 - s0)], BF16, name="grouped", align_bytes=64)
+            nc.scalar.copy(grouped[g][:].bitcast(F32).rearrange("p (c u) -> p c u", u=2), picked[g][:].bitcast(F32).rearrange("p u c -> p c u"))
+
+        def quantize(key, width):
+            codes[key] = keep.tile([P, width], U32, name=f"codes{key}", align_bytes=64)
+            scales[key] = keep.tile([P, width], U8, name=f"scales{key}", align_bytes=64)
+            nc.vector.quantize_mx(out=codes[key][:].bitcast(FP8X4), scales=scales[key][:], in_=grouped[key][:])
+
+        def product(acc, e, h, key, c0, c1):
+            nc.tensor.matmul_mx(
+                out=acc,
+                lhsT=w_sb[:, e, 2 * P * h : 2 * P * (h + 1)].bitcast(FP4X4),
+                lhsT_scale=w_plane[:, e, P * h : P * (h + 1)],
+                rhs=codes[key][:, c0:c1].bitcast(FP8X4),
+                rhs_scale=scales[key][:, c0:c1],
+                start=True,
+                stop=True,
+            )
+
+        def experts(g, h):
+            s0, s1 = SLOT_GROUPS[g]
+            acc = psum_mm.tile([P, s1 - s0], F32, name="acc")
+            for c0 in range(0, s1 - s0, C):
+                product(acc[:, c0 : c0 + C], (s0 + c0) // C, h, g, c0, c0 + C)
+            for c0 in range(0, s1 - s0, C):
+                e = (s0 + c0) // C
+                nc.scalar.activation(y[h][:, s0 + c0 : s0 + c0 + C], acc[:, c0 : c0 + C], GELU, bias=bias[:, h, e : e + 1])
+
+        def shared_interleave(i):
+            t0, t1 = SHARED_GROUPS[i]
+            key = 100 + i
+            grouped[key] = keep.tile([P, PACK * (t1 - t0)], BF16, name=f"shared_grouped{i}", align_bytes=64)
+            words = grouped[key][:].bitcast(F32).rearrange("p (c u) -> p c u", u=2)
+            nc.scalar.copy(words, both[:].bitcast(F32).rearrange("p u c -> p c u")[:, t0:t1, :])
+
+        def shared_expert(i, h):
+            t0, t1 = SHARED_GROUPS[i]
+            acc = psum_mm.tile([P, t1 - t0], F32, name="acc")
+            product(acc[:], E, h, 100 + i, 0, t1 - t0)
+            nc.scalar.activation(ys[h][:, t0:t1], acc[:], GELU, bias=bias[:, h, E : E + 1])
+
+        def combine(h, t0, t1):
+            width = t1 - t0
+            blocks = range(0, width, P)
+            turned = psum_t.tile([P, width], F32, name="turned")
+            for t in blocks:
+                nc.tensor.matmul(turned[:, t : t + P], ys[h][:, t0 + t : t0 + t + P], ident[:], start=(t == 0), stop=False, is_transpose=True)
+            for r in range(TOP):
+                term = ring.tile([P, width], F32, name=f"term{r}")
+                nc.vector.tensor_tensor(term[:], y[h][:].indirect(pos_sb[r][:, t0 // LIST_ROWS : t1 // LIST_ROWS]), gate_sb[h, r][:, t0:t1], MULT)
+                for t in blocks:
+                    nc.tensor.matmul(turned[:, t : t + P], term[:, t : t + P], ident[:], start=False, stop=(r == TOP - 1 and t == width - P), is_transpose=True)
+            turned_sb = ring.tile([P, width], F32, name="turned_sb")
+            nc.scalar.copy(turned_sb[:], turned[:])
+            back = psum_t.tile([P, width], F32, name="back")
+            for t in blocks:
+                nc.tensor.transpose(back[:, t : t + P], turned_sb[:, t : t + P], ident[:])
+            result = ring.tile([P, width], F32, name="result")
+            nc.scalar.copy(result[:], back[:])
+            nc.sync.dma_start(out[h * P : (h + 1) * P, t0:t1], result[:])
+
+        groups = len(SLOT_GROUPS)
+        lead = 3
+        for g in range(lead):
+            gather(g, 0)
+        for g in range(groups):
+            gather(g, 1)
+            interleave(g)
+            quantize(g, SLOT_GROUPS[g][1] - SLOT_GROUPS[g][0])
+            experts(g, 0)
+            if g + lead < groups:
+                gather(g + lead, 0)
+        for i, (t0, t1) in enumerate(SHARED_GROUPS):
+            shared_interleave(i)
+            quantize(100 + i, t1 - t0)
+        for i in range(len(SHARED_GROUPS)):
+            shared_expert(i, 0)
+        for g in range(groups):
+            experts(g, 1)
+        for i in range(len(SHARED_GROUPS)):
+            shared_expert(i, 1)
+        for h in range(HALVES):
+            for t0, t1 in PIECES:
+                combine(h, t0, t1)

@@ -18,6 +18,7 @@ FP8X4 = mybir.dt.float8_e4m3fn_x4
 FP4X4 = mybir.dt.float4_e2m1fn_x4
 GELU = mybir.ActivationFunctionType.Gelu_apprx_tanh
 MULT = mybir.AluOpType.mult
+ADD = mybir.AluOpType.add
 
 P = 128
 PACK = 4
@@ -35,29 +36,26 @@ def spans(widths):
 
 
 X_CHUNKS = spans([512, 512, 256])
-SLOT_GROUPS = spans([512] * 7 + [256])
-SHARED_GROUPS = spans([512, 512, 256])
-PIECES = spans([512, 512, 256])
+GROUPS = spans([768, 768, 512, 512, 512, 512, 256])
+EARLY = (0, 4)
+PIECES = [spans([512, 512, 256]), spans([512, 256])]
 
 
 def tile_moe_shr_lin_gelu_kernel(tc, xT, w_words, w_scales, b, gate, offs, pos1, pos2, pos3, out):
     nc = tc.nc
     with ExitStack() as ctx:
         keep = ctx.enter_context(tc.tile_pool(name="keep", bufs=1))
-        ring = ctx.enter_context(tc.tile_pool(name="ring", bufs=3))
-        stage = ctx.enter_context(tc.tile_pool(name="stage", bufs=6))
-        psum_mm = ctx.enter_context(tc.psum_pool(name="psum_mm", bufs=4))
-        psum_t = ctx.enter_context(tc.psum_pool(name="psum_t", bufs=2))
-
-        offs_sb = keep.tile([P, SLOTS // LIST_ROWS], U16, name="offs_sb")
-        nc.sync.dma_start(offs_sb[:], offs)
+        psum = ctx.enter_context(tc.psum_pool(name="psum", bufs=1))
 
         x_rows = xT.rearrange("(p j) t -> p j t", j=PACK)
         raw = {}
+        offs_sb = keep.tile([P, SLOTS // LIST_ROWS], U16, name="offs_sb")
         for u in range(2):
             for c0, c1 in X_CHUNKS:
-                raw[u, c0] = stage.tile([P, 2, c1 - c0], F32, name="staged")
+                raw[u, c0] = keep.tile([P, 2, c1 - c0], F32, name=f"raw{u}_{c0}", tag=f"room{u}_{c0}", align_bytes=64)
                 nc.sync.dma_start(raw[u, c0][:], x_rows[:, 2 * u : 2 * u + 2, c0:c1])
+            if u == 0:
+                nc.sync.dma_start(offs_sb[:], offs)
 
         w_plane = keep.tile([P, E + 1, N], U8, name="w_plane", align_bytes=64)
         nc.vector.memset(w_plane[:].rearrange("p e n -> p (e n)").bitcast(I32), 0)
@@ -66,10 +64,6 @@ def tile_moe_shr_lin_gelu_kernel(tc, xT, w_words, w_scales, b, gate, offs, pos1,
             nc.sync.dma_start(w_plane[32 * quad : 32 * quad + 4, :, :].bitcast(I32), scale_rows[4 * quad : 4 * quad + 4, :, :].bitcast(I32))
         bias = keep.tile([P, HALVES, E + 1], F32, name="bias")
         nc.sync.dma_start(bias[:], b.rearrange("(h p) e -> p h e", p=P))
-        w_sb = keep.tile([P, E + 1, 2 * N], U8, name="w_sb", align_bytes=64)
-        word_rows = w_words.rearrange("e a p n -> p (e a) n")
-        for e0 in (0, 8):
-            nc.sync.dma_start(w_sb[:, e0 : e0 + 8, :].bitcast(I32), word_rows[:, e0 : e0 + 8, :].bitcast(I32))
         pos_sb = []
         for r, pos in enumerate((pos1, pos2, pos3)):
             tile = keep.tile([P, T // LIST_ROWS], U16, name=f"pos_sb{r}")
@@ -80,9 +74,9 @@ def tile_moe_shr_lin_gelu_kernel(tc, xT, w_words, w_scales, b, gate, offs, pos1,
         make_identity(nc, ident[:])
 
         both = keep.tile([P, 2, 2 * T], BF16, name="both")
-        pairs = [both[:, u, :] for u in range(2)]
+
         def cast(copy, u, c0, t0, t1):
-            copy(pairs[u][:, 2 * t0 : 2 * t1].rearrange("p (t e) -> p t e", e=2), raw[u, c0][:, :, t0 - c0 : t1 - c0].rearrange("p e t -> p t e"))
+            copy(both[:, u, 2 * t0 : 2 * t1].rearrange("p (t e) -> p t e", e=2), raw[u, c0][:, :, t0 - c0 : t1 - c0].rearrange("p e t -> p t e"))
 
         for c0, c1 in X_CHUNKS:
             cut = c0 + 5 * (c1 - c0) // 8
@@ -91,106 +85,168 @@ def tile_moe_shr_lin_gelu_kernel(tc, xT, w_words, w_scales, b, gate, offs, pos1,
         for c0, c1 in X_CHUNKS:
             cast(nc.scalar.copy, 1, c0, c0, c1)
 
+        word_rows = w_words.rearrange("e a p n -> p (e a) n")
+        w_sb = []
+        for i in range(2):
+            tile = keep.tile([P, 8, 2 * N], U8, name=f"w_sb{i}", tag=f"room0_{X_CHUNKS[i][0]}", align_bytes=64)
+            nc.sync.dma_start(tile[:].bitcast(I32), word_rows[:, 8 * i : 8 * i + 8, :].bitcast(I32))
+            w_sb.append(tile)
         gate_sb = {}
-        for h in range(HALVES):
-            for r in range(TOP):
-                gate_sb[h, r] = stage.tile([P, T], F32, name="staged")
-                nc.sync.dma_start(gate_sb[h, r][:], gate[r, h * P : (h + 1) * P, :])
+
+        def load_gate(h, r, room):
+            gate_sb[h, r] = keep.tile([P, T], F32, name=f"gate{h}_{r}", tag=room, align_bytes=64)
+            nc.sync.dma_start(gate_sb[h, r][:], gate[r, h * P : (h + 1) * P, :])
+
+        for h, r, room in ((0, 0, "room0_1024"), (0, 1, "room1_0"), (0, 2, "room1_512"), (1, 0, "room1_1024")):
+            load_gate(h, r, room)
 
         y = [keep.tile([P, SLOTS], F32, name=f"y{h}") for h in range(HALVES)]
         ys = [keep.tile([P, T], F32, name=f"ys{h}") for h in range(HALVES)]
+        terms = {(h, r): keep.tile([P, T], F32, name=f"term{h}_{r}") for h in range(HALVES) for r in range(TOP)}
+        banks = [psum.tile([P, BANK], F32, name=f"bank{i}") for i in range(8)]
+        codes = keep.tile([P, SLOTS + T], U32, name="codes", align_bytes=64)
+        scales = keep.tile([P, SLOTS + T], U8, name="scales", align_bytes=64)
 
-        picked, grouped, codes, scales = {}, {}, {}, {}
+        shared = keep.tile([P, PACK * 1024], BF16, name="shared", align_bytes=64)
+        odd = keep.tile([P, PACK * 768], BF16, name="odd", tag="odd", align_bytes=64)
+        grouped = keep.tile([P, PACK * 768], BF16, name="grouped", tag="grouped", align_bytes=64)
+
+        def picked(g):
+            width = PACK * (GROUPS[g][1] - GROUPS[g][0])
+            room = shared if g % 2 == 0 else odd
+            return room[:, room.shape[1] - width :].rearrange("p (u c) -> p u c", u=2)
 
         def gather(g, u):
-            s0, s1 = SLOT_GROUPS[g]
-            if u == 0:
-                picked[g] = ring.tile([P, 2, 2 * (s1 - s0)], BF16, name="picked")
-            nc.vector.tensor_copy(picked[g][:, u, :].bitcast(U32), pairs[u].bitcast(U32).indirect(offs_sb[:, s0 // LIST_ROWS : s1 // LIST_ROWS]))
+            s0, s1 = GROUPS[g]
+            nc.vector.tensor_copy(picked(g)[:, u, :].bitcast(U32), both[:, u, :].bitcast(U32).indirect(offs_sb[:, s0 // LIST_ROWS : s1 // LIST_ROWS]))
 
-        def interleave(g):
-            s0, s1 = SLOT_GROUPS[g]
-            grouped[g] = ring.tile([P, PACK * (s1 - s0)], BF16, name="grouped", align_bytes=64)
-            nc.scalar.copy(grouped[g][:].bitcast(F32).rearrange("p (c u) -> p c u", u=2), picked[g][:].bitcast(F32).rearrange("p u c -> p c u"))
+        def interleave(dst, planes):
+            nc.scalar.copy(dst.bitcast(F32).rearrange("p (c u) -> p c u", u=2), planes.bitcast(F32).rearrange("p u c -> p c u"))
 
-        def quantize(key, width):
-            codes[key] = keep.tile([P, width], U32, name=f"codes{key}", align_bytes=64)
-            scales[key] = keep.tile([P, width], U8, name=f"scales{key}", align_bytes=64)
-            nc.vector.quantize_mx(out=codes[key][:].bitcast(FP8X4), scales=scales[key][:], in_=grouped[key][:])
+        def quantize(src, c0, c1):
+            nc.vector.quantize_mx(out=codes[:, c0:c1].bitcast(FP8X4), scales=scales[:, c0:c1], in_=src)
 
-        def product(acc, e, h, key, c0, c1):
+        def expert(bank, at, e, h, c0, c1, dst):
+            acc = bank[:, at : at + c1 - c0]
             nc.tensor.matmul_mx(
                 out=acc,
-                lhsT=w_sb[:, e, 2 * P * h : 2 * P * (h + 1)].bitcast(FP4X4),
+                lhsT=w_sb[e // 8][:, e % 8, 2 * P * h : 2 * P * (h + 1)].bitcast(FP4X4),
                 lhsT_scale=w_plane[:, e, P * h : P * (h + 1)],
-                rhs=codes[key][:, c0:c1].bitcast(FP8X4),
-                rhs_scale=scales[key][:, c0:c1],
+                rhs=codes[:, c0:c1].bitcast(FP8X4),
+                rhs_scale=scales[:, c0:c1],
                 start=True,
                 stop=True,
             )
+            return lambda: nc.scalar.activation(dst, acc, GELU, bias=bias[:, h, e : e + 1])
 
-        def experts(g, h):
-            s0, s1 = SLOT_GROUPS[g]
-            acc = psum_mm.tile([P, s1 - s0], F32, name="acc")
-            for c0 in range(0, s1 - s0, C):
-                product(acc[:, c0 : c0 + C], (s0 + c0) // C, h, g, c0, c0 + C)
-            for c0 in range(0, s1 - s0, C):
-                e = (s0 + c0) // C
-                nc.scalar.activation(y[h][:, s0 + c0 : s0 + c0 + C], acc[:, c0 : c0 + C], GELU, bias=bias[:, h, e : e + 1])
+        def place(s):
+            return s + 768 if s < 768 else s
 
-        def shared_interleave(i):
-            t0, t1 = SHARED_GROUPS[i]
-            key = 100 + i
-            grouped[key] = keep.tile([P, PACK * (t1 - t0)], BF16, name=f"shared_grouped{i}", align_bytes=64)
-            words = grouped[key][:].bitcast(F32).rearrange("p (c u) -> p c u", u=2)
-            nc.scalar.copy(words, both[:].bitcast(F32).rearrange("p u c -> p c u")[:, t0:t1, :])
+        def routed(bank, h, experts):
+            gelus = [expert(bank, i * C, e, h, place(e * C), place(e * C) + C, y[h][:, e * C : (e + 1) * C]) for i, e in enumerate(experts)]
+            for gelu in gelus:
+                gelu()
 
-        def shared_expert(i, h):
-            t0, t1 = SHARED_GROUPS[i]
-            acc = psum_mm.tile([P, t1 - t0], F32, name="acc")
-            product(acc[:], E, h, 100 + i, 0, t1 - t0)
-            nc.scalar.activation(ys[h][:, t0:t1], acc[:], GELU, bias=bias[:, h, E : E + 1])
+        def in_twos(experts):
+            return [experts[i : i + 2] for i in range(0, len(experts), 2)]
 
-        def combine(h, t0, t1):
+        def shared_expert(bank, h, t0, t1):
+            expert(bank, 0, E, h, SLOTS + t0, SLOTS + t1, ys[h][:, t0:t1])()
+
+        turns = []
+
+        def next_bank():
+            turns.append(len(turns) % 4)
+            return banks[turns[-1]]
+
+        def weigh(h, r, t0, t1):
+            nc.vector.tensor_tensor(terms[h, r][:, t0:t1], y[h][:].indirect(pos_sb[r][:, t0 // LIST_ROWS : t1 // LIST_ROWS]), gate_sb[h, r][:, t0:t1], MULT)
+
+        def add_up(addends, t0, t1, turned, through, back):
             width = t1 - t0
             blocks = range(0, width, P)
-            turned = psum_t.tile([P, width], F32, name="turned")
-            for t in blocks:
-                nc.tensor.matmul(turned[:, t : t + P], ys[h][:, t0 + t : t0 + t + P], ident[:], start=(t == 0), stop=False, is_transpose=True)
-            for r in range(TOP):
-                term = ring.tile([P, width], F32, name=f"term{r}")
-                nc.vector.tensor_tensor(term[:], y[h][:].indirect(pos_sb[r][:, t0 // LIST_ROWS : t1 // LIST_ROWS]), gate_sb[h, r][:, t0:t1], MULT)
+            for a, addend in enumerate(addends):
                 for t in blocks:
-                    nc.tensor.matmul(turned[:, t : t + P], term[:, t : t + P], ident[:], start=False, stop=(r == TOP - 1 and t == width - P), is_transpose=True)
-            turned_sb = ring.tile([P, width], F32, name="turned_sb")
-            nc.scalar.copy(turned_sb[:], turned[:])
-            back = psum_t.tile([P, width], F32, name="back")
+                    nc.tensor.matmul(
+                        turned[:, t : t + P],
+                        addend[:, t0 + t : t0 + t + P],
+                        ident[:],
+                        start=(a == 0 and t == 0),
+                        stop=(a == len(addends) - 1 and t == width - P),
+                        is_transpose=True,
+                    )
+            nc.scalar.copy(through[:, 0:width], turned[:, 0:width])
             for t in blocks:
-                nc.tensor.transpose(back[:, t : t + P], turned_sb[:, t : t + P], ident[:])
-            result = ring.tile([P, width], F32, name="result")
-            nc.scalar.copy(result[:], back[:])
-            nc.sync.dma_start(out[h * P : (h + 1) * P, t0:t1], result[:])
+                nc.tensor.transpose(back[:, t : t + P], through[:, t : t + P], ident[:])
 
-        groups = len(SLOT_GROUPS)
-        lead = 3
-        for g in range(lead):
-            gather(g, 0)
-        for g in range(groups):
-            gather(g, 1)
-            interleave(g)
-            quantize(g, SLOT_GROUPS[g][1] - SLOT_GROUPS[g][0])
-            experts(g, 0)
-            if g + lead < groups:
-                gather(g + lead, 0)
-        for i, (t0, t1) in enumerate(SHARED_GROUPS):
-            shared_interleave(i)
-            quantize(100 + i, t1 - t0)
-        for i in range(len(SHARED_GROUPS)):
-            shared_expert(i, 0)
-        for g in range(groups):
-            experts(g, 1)
-        for i in range(len(SHARED_GROUPS)):
-            shared_expert(i, 1)
-        for h in range(HALVES):
-            for t0, t1 in PIECES:
-                combine(h, t0, t1)
+        def combine(i, h, t0, t1):
+            for r in range(TOP):
+                weigh(h, r, t0, t1)
+            add_up([terms[h, 0], terms[h, 1], ys[h], terms[h, 2]], t0, t1, banks[4 + i % 2], turned_sb[i % 2], banks[6 + i % 2])
+            nc.scalar.copy(result[h][:, t0:t1], banks[6 + i % 2][:, 0 : t1 - t0])
+            nc.sync.dma_start(out[h * P : (h + 1) * P, t0:t1], result[h][:, t0:t1])
+
+        turned_sb = [keep.tile([P, BANK], F32, name=f"turned_sb{i}") for i in range(3)]
+        result = [keep.tile([P, T], F32, name=f"result{h}") for h in range(HALVES)]
+
+        def shared_interleave(dst, t0, t1):
+            interleave(dst, both[:, :, 2 * t0 : 2 * t1])
+
+        last = len(GROUPS) - 1
+        for u in range(2):
+            for g in range(2):
+                gather(g, u)
+        for g, (s0, s1) in enumerate(GROUPS):
+            for c0 in range(0, s1 - s0, BANK):
+                c1 = min(c0 + BANK, s1 - s0)
+                at = BANK if g == last else c0
+                room = shared[:, 0 : PACK * 256] if (g, c0) == (0, BANK) else grouped[:, PACK * at : PACK * (at + c1 - c0)]
+                interleave(room, picked(g)[:, :, 2 * c0 : 2 * c1])
+                quantize(room, place(s0 + c0), place(s0 + c0) + c1 - c0)
+            if g + 2 <= last:
+                gather(g + 2, 0)
+                gather(g + 2, 1)
+            experts = list(range(s0 // C, s1 // C))
+            if g < last:
+                for h in range(HALVES if g in EARLY else 1):
+                    for two in in_twos(experts):
+                        routed(next_bank(), h, two)
+            if g == 0:
+                shared_interleave(shared[:, 0 : PACK * 512], 0, 512)
+            if g == 1:
+                shared_interleave(odd[:, 0 : PACK * 256], 1024, T)
+                quantize(odd[:, 0 : PACK * 256], SLOTS + 1024, SLOTS + T)
+                for h in range(HALVES):
+                    shared_expert(next_bank(), h, 1024, T)
+            if g == last - 2:
+                shared_interleave(shared[:, PACK * 512 : PACK * 768], 512, 768)
+        closing = [next_bank(), next_bank()]
+        gelus = [expert(closing[i], 0, E - 1, 0, SLOTS - C + i * P, SLOTS - C + (i + 1) * P, y[0][:, SLOTS - C + i * P : SLOTS - C + (i + 1) * P]) for i in range(2)]
+        for gelu in gelus:
+            gelu()
+
+        shared_interleave(shared[:, PACK * 768 : PACK * 1024], 768, 1024)
+        quantize(shared[:], SLOTS, SLOTS + 1024)
+        load_gate(1, 1, "odd")
+        load_gate(1, 2, "grouped")
+        spare = [next_bank(), next_bank()]
+        for i in range(2):
+            shared_expert(spare[i], 0, i * BANK, (i + 1) * BANK)
+        deferred = [e for g, (s0, s1) in enumerate(GROUPS) if g not in EARLY for e in range(s0 // C, s1 // C)]
+        for i, two in enumerate(in_twos(deferred)):
+            routed(closing[i % 2], 1, two)
+        for t0 in (0, 512):
+            shared_expert(next_bank(), 1, t0, t0 + 512)
+        for i, (t0, t1) in enumerate(PIECES[0]):
+            combine(i, 0, t0, t1)
+        for r in range(TOP - 1):
+            weigh(1, r, T - BANK, T)
+        add_up([terms[1, 0], ys[1], terms[1, 1]], T - BANK, T, spare[0], turned_sb[2], spare[1])
+        for i, (t0, t1) in enumerate(PIECES[1], len(PIECES[0])):
+            combine(i, 1, t0, t1)
+        ending = ((T - BANK, T - 256), (T - 256, T))
+        for t0, t1 in ending:
+            weigh(1, TOP - 1, t0, t1)
+        for t0, t1 in ending:
+            nc.vector.tensor_tensor(result[1][:, t0:t1], spare[1][:, t0 - T + BANK : t1 - T + BANK], terms[1, TOP - 1][:, t0:t1], ADD)
+            nc.sync.dma_start(out[P : 2 * P, t0:t1], result[1][:, t0:t1])

@@ -37,8 +37,8 @@ def spans(widths):
 
 X_CHUNKS = spans([512, 512, 256])
 GROUPS = spans([768, 768, 512, 512, 512, 512, 256])
-EARLY = (0, 4)
-PIECES = [spans([512, 512, 256]), spans([512, 256])]
+EARLY = (0, 2, 3, 4)
+PIECES = [spans([512, 512, 256]), spans([512, 512, 256])]
 
 
 def tile_moe_shr_lin_gelu_kernel(tc, xT, w_words, w_scales, b, gate, offs, pos1, pos2, pos3, out):
@@ -88,8 +88,8 @@ def tile_moe_shr_lin_gelu_kernel(tc, xT, w_words, w_scales, b, gate, offs, pos1,
         word_rows = w_words.rearrange("e a p n -> p (e a) n")
         w_sb = []
         for i in range(2):
-            tile = keep.tile([P, 8, 2 * N], U8, name=f"w_sb{i}", tag=f"room0_{X_CHUNKS[i][0]}", align_bytes=64)
-            nc.sync.dma_start(tile[:].bitcast(I32), word_rows[:, 8 * i : 8 * i + 8, :].bitcast(I32))
+            tile = keep.tile([P, 8, 4 * N], U8, name=f"w_sb{i}", tag=f"room0_{X_CHUNKS[i][0]}", align_bytes=64)
+            nc.sync.dma_start(tile[:, :, 2 * N :].bitcast(I32), word_rows[:, 8 * i : 8 * i + 8, :].bitcast(I32))
             w_sb.append(tile)
         gate_sb = {}
 
@@ -107,14 +107,31 @@ def tile_moe_shr_lin_gelu_kernel(tc, xT, w_words, w_scales, b, gate, offs, pos1,
         codes = keep.tile([P, SLOTS + T], U32, name="codes", align_bytes=64)
         scales = keep.tile([P, SLOTS + T], U8, name="scales", align_bytes=64)
 
-        shared = keep.tile([P, PACK * 1024], BF16, name="shared", align_bytes=64)
-        odd = keep.tile([P, PACK * 768], BF16, name="odd", tag="odd", align_bytes=64)
-        grouped = keep.tile([P, PACK * 768], BF16, name="grouped", tag="grouped", align_bytes=64)
+        even = keep.tile([P, 2 * PACK * 1024], BF16, name="even", align_bytes=64)
+        small = keep.tile([P, PACK * 256], BF16, name="small", align_bytes=64)
+        odd = keep.tile([P, PACK * 1536], BF16, name="odd", tag="odd", align_bytes=64)
+        grouped = keep.tile([P, PACK * 1024], BF16, name="grouped", tag="grouped", align_bytes=64)
+
+        shared = even[:, 4096:]
 
         def picked(g):
-            width = PACK * (GROUPS[g][1] - GROUPS[g][0])
-            room = shared if g % 2 == 0 else odd
-            return room[:, room.shape[1] - width :].rearrange("p (u c) -> p u c", u=2)
+            plane = 2 * (GROUPS[g][1] - GROUPS[g][0])
+            start, step = {0: (1024, 1536), 1: (0, 1536), 2: (0, 3072), 3: (2048, 1024), 4: (0, 3072), 5: (2048, 1024), 6: (3200, 512)}[g]
+            return (odd if g % 2 else even)[:, start : start + 2 * step].rearrange("p (u c) -> p u c", u=2)[:, :, 0:plane]
+
+        def room_of(g, c0):
+            rooms = {
+                (0, 0): grouped[:, 0:2048],
+                (0, BANK): grouped[:, 2048:3072],
+                (1, 0): odd[:, 3072:5120],
+                (1, BANK): grouped[:, 3072:4096],
+                (2, 0): odd[:, 4096:6144],
+                (3, 0): odd[:, 4096:6144],
+                (4, 0): odd[:, 4096:6144],
+                (5, 0): grouped[:, 0:2048],
+                (6, 0): grouped[:, 2048:3072],
+            }
+            return rooms[g, c0]
 
         def gather(g, u):
             s0, s1 = GROUPS[g]
@@ -123,24 +140,33 @@ def tile_moe_shr_lin_gelu_kernel(tc, xT, w_words, w_scales, b, gate, offs, pos1,
         def interleave(dst, planes):
             nc.scalar.copy(dst.bitcast(F32).rearrange("p (c u) -> p c u", u=2), planes.bitcast(F32).rearrange("p u c -> p c u"))
 
+        def scale_bytes(c0, c1):
+            for s0, s1 in GROUPS[1:2]:
+                end = min(s0 + BANK, s1)
+                if s0 <= c0 < end:
+                    e = s0 // C - 1
+                    first = 2 * N + 64 - (end - s0)
+                    return w_sb[e // 8][:, e % 8, first + c0 - s0 : first + c1 - s0]
+            return scales[:, c0:c1]
+
         def quantize(src, c0, c1):
-            nc.vector.quantize_mx(out=codes[:, c0:c1].bitcast(FP8X4), scales=scales[:, c0:c1], in_=src)
+            nc.vector.quantize_mx(out=codes[:, c0:c1].bitcast(FP8X4), scales=scale_bytes(c0, c1), in_=src)
 
         def expert(bank, at, e, h, c0, c1, dst):
             acc = bank[:, at : at + c1 - c0]
             nc.tensor.matmul_mx(
                 out=acc,
-                lhsT=w_sb[e // 8][:, e % 8, 2 * P * h : 2 * P * (h + 1)].bitcast(FP4X4),
+                lhsT=w_sb[e // 8][:, e % 8, 2 * N + 2 * P * h : 2 * N + 2 * P * (h + 1)].bitcast(FP4X4),
                 lhsT_scale=w_plane[:, e, P * h : P * (h + 1)],
                 rhs=codes[:, c0:c1].bitcast(FP8X4),
-                rhs_scale=scales[:, c0:c1],
+                rhs_scale=scale_bytes(c0, c1),
                 start=True,
                 stop=True,
             )
             return lambda: nc.scalar.activation(dst, acc, GELU, bias=bias[:, h, e : e + 1])
 
         def place(s):
-            return s + 768 if s < 768 else s
+            return s
 
         def routed(bank, h, experts):
             gelus = [expert(bank, i * C, e, h, place(e * C), place(e * C) + C, y[h][:, e * C : (e + 1) * C]) for i, e in enumerate(experts)]
@@ -162,71 +188,68 @@ def tile_moe_shr_lin_gelu_kernel(tc, xT, w_words, w_scales, b, gate, offs, pos1,
         def weigh(h, r, t0, t1):
             nc.vector.tensor_tensor(terms[h, r][:, t0:t1], y[h][:].indirect(pos_sb[r][:, t0 // LIST_ROWS : t1 // LIST_ROWS]), gate_sb[h, r][:, t0:t1], MULT)
 
-        def add_up(addends, t0, t1, turned, through, back):
-            width = t1 - t0
-            blocks = range(0, width, P)
+        def turn(addend, t0, t1, bank, opens, closes):
+            for t in range(t0, t1, P):
+                nc.tensor.matmul(
+                    bank[:, t - t0 : t - t0 + P],
+                    addend[:, t : t + P],
+                    ident[:],
+                    start=(opens and t == t0),
+                    stop=(closes and t == t1 - P),
+                    is_transpose=True,
+                )
+
+        def add_up(h, count, t0, t1, turned, through, back):
+            opened = t0 == 2 * BANK
+            addends = [terms[h, r] for r in range(count)]
+            if not opened:
+                addends.insert(count - 1, ys[h])
             for a, addend in enumerate(addends):
-                for t in blocks:
-                    nc.tensor.matmul(
-                        turned[:, t : t + P],
-                        addend[:, t0 + t : t0 + t + P],
-                        ident[:],
-                        start=(a == 0 and t == 0),
-                        stop=(a == len(addends) - 1 and t == width - P),
-                        is_transpose=True,
-                    )
-            nc.scalar.copy(through[:, 0:width], turned[:, 0:width])
-            for t in blocks:
+                turn(addend, t0, t1, turned, a == 0 and not opened, a == len(addends) - 1)
+            nc.scalar.copy(through[:, 0 : t1 - t0], turned[:, 0 : t1 - t0])
+            for t in range(0, t1 - t0, P):
                 nc.tensor.transpose(back[:, t : t + P], through[:, t : t + P], ident[:])
 
-        def combine(i, h, t0, t1):
-            for r in range(TOP):
-                weigh(h, r, t0, t1)
-            add_up([terms[h, 0], terms[h, 1], ys[h], terms[h, 2]], t0, t1, banks[4 + i % 2], turned_sb[i % 2], banks[6 + i % 2])
-            nc.scalar.copy(result[h][:, t0:t1], banks[6 + i % 2][:, 0 : t1 - t0])
-            nc.sync.dma_start(out[h * P : (h + 1) * P, t0:t1], result[h][:, t0:t1])
-
-        turned_sb = [keep.tile([P, BANK], F32, name=f"turned_sb{i}") for i in range(3)]
+        turned_sb = [keep.tile([P, BANK], F32, name=f"turned_sb{i}") for i in range(4)]
         result = [keep.tile([P, T], F32, name=f"result{h}") for h in range(HALVES)]
 
         def shared_interleave(dst, t0, t1):
             interleave(dst, both[:, :, 2 * t0 : 2 * t1])
 
         last = len(GROUPS) - 1
-        for u in range(2):
-            for g in range(2):
-                gather(g, u)
+        for g in range(3):
+            gather(g, 0)
+        for g in range(2):
+            gather(g, 1)
+        shared_interleave(shared[:, PACK * 32 :], 32, 1024)
+        shared_interleave(small[:], 1024, T)
+        quantize(small[:], SLOTS + 1024, SLOTS + T)
         for g, (s0, s1) in enumerate(GROUPS):
             for c0 in range(0, s1 - s0, BANK):
                 c1 = min(c0 + BANK, s1 - s0)
-                at = BANK if g == last else c0
-                room = shared[:, 0 : PACK * 256] if (g, c0) == (0, BANK) else grouped[:, PACK * at : PACK * (at + c1 - c0)]
+                room = room_of(g, c0)
                 interleave(room, picked(g)[:, :, 2 * c0 : 2 * c1])
                 quantize(room, place(s0 + c0), place(s0 + c0) + c1 - c0)
             if g + 2 <= last:
-                gather(g + 2, 0)
+                if g > 0:
+                    gather(g + 2, 0)
                 gather(g + 2, 1)
             experts = list(range(s0 // C, s1 // C))
             if g < last:
                 for h in range(HALVES if g in EARLY else 1):
                     for two in in_twos(experts):
                         routed(next_bank(), h, two)
-            if g == 0:
-                shared_interleave(shared[:, 0 : PACK * 512], 0, 512)
-            if g == 1:
-                shared_interleave(odd[:, 0 : PACK * 256], 1024, T)
-                quantize(odd[:, 0 : PACK * 256], SLOTS + 1024, SLOTS + T)
+            if g == 2:
                 for h in range(HALVES):
-                    shared_expert(next_bank(), h, 1024, T)
-            if g == last - 2:
-                shared_interleave(shared[:, PACK * 512 : PACK * 768], 512, 768)
+                    shared_expert(next_bank(), h, 2 * BANK, T)
+                    turn(ys[h], 2 * BANK, T, banks[6 + h], True, False)
         closing = [next_bank(), next_bank()]
         gelus = [expert(closing[i], 0, E - 1, 0, SLOTS - C + i * P, SLOTS - C + (i + 1) * P, y[0][:, SLOTS - C + i * P : SLOTS - C + (i + 1) * P]) for i in range(2)]
         for gelu in gelus:
             gelu()
 
-        shared_interleave(shared[:, PACK * 768 : PACK * 1024], 768, 1024)
-        quantize(shared[:], SLOTS, SLOTS + 1024)
+        shared_interleave(shared[:, 0 : PACK * 32], 0, 32)
+        quantize(shared, SLOTS, SLOTS + 1024)
         load_gate(1, 1, "odd")
         load_gate(1, 2, "grouped")
         spare = [next_bank(), next_bank()]
@@ -235,18 +258,22 @@ def tile_moe_shr_lin_gelu_kernel(tc, xT, w_words, w_scales, b, gate, offs, pos1,
         deferred = [e for g, (s0, s1) in enumerate(GROUPS) if g not in EARLY for e in range(s0 // C, s1 // C)]
         for i, two in enumerate(in_twos(deferred)):
             routed(closing[i % 2], 1, two)
-        for t0 in (0, 512):
-            shared_expert(next_bank(), 1, t0, t0 + 512)
+        for i in range(2):
+            shared_expert(closing[i], 1, i * BANK, (i + 1) * BANK)
         for i, (t0, t1) in enumerate(PIECES[0]):
-            combine(i, 0, t0, t1)
-        for r in range(TOP - 1):
-            weigh(1, r, T - BANK, T)
-        add_up([terms[1, 0], ys[1], terms[1, 1]], T - BANK, T, spare[0], turned_sb[2], spare[1])
-        for i, (t0, t1) in enumerate(PIECES[1], len(PIECES[0])):
-            combine(i, 1, t0, t1)
-        ending = ((T - BANK, T - 256), (T - 256, T))
-        for t0, t1 in ending:
+            for r in range(TOP):
+                weigh(0, r, t0, t1)
+            add_up(0, TOP, t0, t1, banks[4 + i], turned_sb[i % 2], spare[i % 2])
+            nc.scalar.copy(result[0][:, t0:t1], spare[i % 2][:, 0 : t1 - t0])
+            nc.sync.dma_start(out[0:P, t0:t1], result[0][:, t0:t1])
+        held = [closing[0], closing[1], banks[6]]
+        for i, (t0, t1) in enumerate(PIECES[0]):
+            for r in range(TOP - 1):
+                weigh(1, r, t0, t1)
+            add_up(1, TOP - 1, t0, t1, banks[(4, 5, 7)[i]], turned_sb[2 + i % 2], held[i])
+        for t0, t1 in PIECES[1]:
             weigh(1, TOP - 1, t0, t1)
-        for t0, t1 in ending:
-            nc.vector.tensor_tensor(result[1][:, t0:t1], spare[1][:, t0 - T + BANK : t1 - T + BANK], terms[1, TOP - 1][:, t0:t1], ADD)
+        for t0, t1 in PIECES[1]:
+            at = t0 % BANK
+            nc.vector.tensor_tensor(result[1][:, t0:t1], held[t0 // BANK][:, at : at + t1 - t0], terms[1, TOP - 1][:, t0:t1], ADD)
             nc.sync.dma_start(out[P : 2 * P, t0:t1], result[1][:, t0:t1])

from contextlib import ExitStack

import concourse.mybir as mybir
from concourse.masks import make_identity

K, T, E, C, N = 512, 1280, 15, 256, 256
TOP = 3
SLOTS = E * C
FLOPS = 2 * K * N * (SLOTS + T)

F32 = mybir.dt.float32
BF16 = mybir.dt.bfloat16
I32 = mybir.dt.int32
U32 = mybir.dt.uint32
U16 = mybir.dt.uint16
U8 = mybir.dt.uint8
FP8X4 = mybir.dt.float8_e4m3fn_x4
FP4X4 = mybir.dt.float4_e2m1fn_x4
GELU = mybir.ActivationFunctionType.Gelu_apprx_tanh
MULT = mybir.AluOpType.mult
ADD = mybir.AluOpType.add

P = 128
PACK = 4
HALVES = N // P
LIST_ROWS = 16
BANK = 512


def spans(widths):
    out, at = [], 0
    for w in widths:
        out.append((at, at + w))
        at += w
    return out


X_CHUNKS = spans([512, 512, 256])
GROUPS = spans([768, 768, 512, 512, 512, 512, 256])
EARLY = (0, 2, 3, 4)
PIECES = [spans([512, 512, 256]), spans([512, 512, 256])]


def tile_moe_shr_lin_gelu_kernel(tc, xT, w_words, w_scales, b, gate, offs, pos1, pos2, pos3, out):
    nc = tc.nc
    with ExitStack() as ctx:
        keep = ctx.enter_context(tc.tile_pool(name="keep", bufs=1))
        psum = ctx.enter_context(tc.psum_pool(name="psum", bufs=1))

        x_rows = xT.rearrange("(p j) t -> p j t", j=PACK)
        raw = {}
        offs_sb = keep.tile([P, SLOTS // LIST_ROWS], U16, name="offs_sb")
        for u in range(2):
            for c0, c1 in X_CHUNKS:
                raw[u, c0] = keep.tile([P, 2, c1 - c0], F32, name=f"raw{u}_{c0}", tag=f"room{u}_{c0}", align_bytes=64)
                nc.sync.dma_start(raw[u, c0][:], x_rows[:, 2 * u : 2 * u + 2, c0:c1])
            if u == 0:
                nc.sync.dma_start(offs_sb[:], offs)

        w_plane = keep.tile([P, E + 1, N], U8, name="w_plane", align_bytes=64)
        nc.vector.memset(w_plane[:].rearrange("p e n -> p (e n)").bitcast(I32), 0)
        scale_rows = w_scales.rearrange("e a q n -> (a q) e n")
        for quad in range(4):
            nc.sync.dma_start(w_plane[32 * quad : 32 * quad + 4, :, :].bitcast(I32), scale_rows[4 * quad : 4 * quad + 4, :, :].bitcast(I32))
        bias = keep.tile([P, HALVES, E + 1], F32, name="bias")
        nc.sync.dma_start(bias[:], b.rearrange("(h p) e -> p h e", p=P))
        pos_sb = []
        for r, pos in enumerate((pos1, pos2, pos3)):
            tile = keep.tile([P, T // LIST_ROWS], U16, name=f"pos_sb{r}")
            nc.sync.dma_start(tile[:], pos)
            pos_sb.append(tile)

        ident = keep.tile([P, P], F32, name="ident")
        make_identity(nc, ident[:])

        both = keep.tile([P, 2, 2 * T], BF16, name="both")

        def cast(copy, u, c0, t0, t1):
            copy(both[:, u, 2 * t0 : 2 * t1].rearrange("p (t e) -> p t e", e=2), raw[u, c0][:, :, t0 - c0 : t1 - c0].rearrange("p e t -> p t e"))

        for c0, c1 in X_CHUNKS:
            cut = c0 + 5 * (c1 - c0) // 8
            cast(nc.vector.tensor_copy, 0, c0, c0, cut)
            cast(nc.scalar.copy, 0, c0, cut, c1)
        for c0, c1 in X_CHUNKS:
            cast(nc.scalar.copy, 1, c0, c0, c1)

        word_rows = w_words.rearrange("e a p n -> p (e a) n")
        w_sb = []
        for i in range(2):
            tile = keep.tile([P, 8, 4 * N], U8, name=f"w_sb{i}", tag=f"room0_{X_CHUNKS[i][0]}", align_bytes=64)
            nc.sync.dma_start(tile[:, :, 2 * N :].bitcast(I32), word_rows[:, 8 * i : 8 * i + 8, :].bitcast(I32))
            w_sb.append(tile)
        gate_sb = {}

        def load_gate(h, r, room):
            gate_sb[h, r] = keep.tile([P, T], F32, name=f"gate{h}_{r}", tag=room, align_bytes=64)
            nc.sync.dma_start(gate_sb[h, r][:], gate[r, h * P : (h + 1) * P, :])

        for h, r, room in ((0, 0, "room0_1024"), (0, 1, "room1_0"), (0, 2, "room1_512"), (1, 0, "room1_1024")):
            load_gate(h, r, room)

        y = [keep.tile([P, SLOTS], F32, name=f"y{h}") for h in range(HALVES)]
        ys = [keep.tile([P, T], F32, name=f"ys{h}") for h in range(HALVES)]
        terms = {(h, r): keep.tile([P, T], F32, name=f"term{h}_{r}") for h in range(HALVES) for r in range(TOP)}
        banks = [psum.tile([P, BANK], F32, name=f"bank{i}") for i in range(8)]
        codes = keep.tile([P, SLOTS + T], U32, name="codes", align_bytes=64)
        scales = keep.tile([P, SLOTS + T], U8, name="scales", align_bytes=64)

        even = keep.tile([P, 2 * PACK * 1024], BF16, name="even", align_bytes=64)
        small = keep.tile([P, PACK * 256], BF16, name="small", align_bytes=64)
        odd = keep.tile([P, PACK * 1536], BF16, name="odd", tag="odd", align_bytes=64)
        grouped = keep.tile([P, PACK * 1024], BF16, name="grouped", tag="grouped", align_bytes=64)

        shared = even[:, 4096:]

        def picked(g):
            plane = 2 * (GROUPS[g][1] - GROUPS[g][0])
            start, step = {0: (1024, 1536), 1: (0, 1536), 2: (0, 3072), 3: (2048, 1024), 4: (0, 3072), 5: (2048, 1024), 6: (3200, 512)}[g]
            return (odd if g % 2 else even)[:, start : start + 2 * step].rearrange("p (u c) -> p u c", u=2)[:, :, 0:plane]

        def room_of(g, c0):
            rooms = {
                (0, 0): grouped[:, 0:2048],
                (0, BANK): grouped[:, 2048:3072],
                (1, 0): odd[:, 3072:5120],
                (1, BANK): grouped[:, 3072:4096],
                (2, 0): odd[:, 4096:6144],
                (3, 0): odd[:, 4096:6144],
                (4, 0): odd[:, 4096:6144],
                (5, 0): grouped[:, 0:2048],
                (6, 0): grouped[:, 2048:3072],
            }
            return rooms[g, c0]

        def gather(g, u):
            s0, s1 = GROUPS[g]
            nc.vector.tensor_copy(picked(g)[:, u, :].bitcast(U32), both[:, u, :].bitcast(U32).indirect(offs_sb[:, s0 // LIST_ROWS : s1 // LIST_ROWS]))

        def interleave(dst, planes):
            nc.scalar.copy(dst.bitcast(F32).rearrange("p (c u) -> p c u", u=2), planes.bitcast(F32).rearrange("p u c -> p c u"))

        def scale_bytes(c0, c1):
            for s0, s1 in GROUPS[1:2]:
                end = min(s0 + BANK, s1)
                if s0 <= c0 < end:
                    e = s0 // C - 1
                    first = 2 * N + 64 - (end - s0)
                    return w_sb[e // 8][:, e % 8, first + c0 - s0 : first + c1 - s0]
            return scales[:, c0:c1]

        def quantize(src, c0, c1):
            nc.vector.quantize_mx(out=codes[:, c0:c1].bitcast(FP8X4), scales=scale_bytes(c0, c1), in_=src)

        def expert(bank, at, e, h, c0, c1, dst):
            acc = bank[:, at : at + c1 - c0]
            nc.tensor.matmul_mx(
                out=acc,
                lhsT=w_sb[e // 8][:, e % 8, 2 * N + 2 * P * h : 2 * N + 2 * P * (h + 1)].bitcast(FP4X4),
                lhsT_scale=w_plane[:, e, P * h : P * (h + 1)],
                rhs=codes[:, c0:c1].bitcast(FP8X4),
                rhs_scale=scale_bytes(c0, c1),
                start=True,
                stop=True,
            )
            return lambda: nc.scalar.activation(dst, acc, GELU, bias=bias[:, h, e : e + 1])

        def place(s):
            return s

        def routed(bank, h, experts):
            gelus = [expert(bank, i * C, e, h, place(e * C), place(e * C) + C, y[h][:, e * C : (e + 1) * C]) for i, e in enumerate(experts)]
            for gelu in gelus:
                gelu()

        def in_twos(experts):
            return [experts[i : i + 2] for i in range(0, len(experts), 2)]

        def shared_expert(bank, h, t0, t1):
            expert(bank, 0, E, h, SLOTS + t0, SLOTS + t1, ys[h][:, t0:t1])()

        turns = []

        def next_bank():
            turns.append(len(turns) % 4)
            return banks[turns[-1]]

        def weigh(h, r, t0, t1):
            nc.vector.tensor_tensor(terms[h, r][:, t0:t1], y[h][:].indirect(pos_sb[r][:, t0 // LIST_ROWS : t1 // LIST_ROWS]), gate_sb[h, r][:, t0:t1], MULT)

        def turn(addend, t0, t1, bank, opens, closes):
            for t in range(t0, t1, P):
                nc.tensor.matmul(
                    bank[:, t - t0 : t - t0 + P],
                    addend[:, t : t + P],
                    ident[:],
                    start=(opens and t == t0),
                    stop=(closes and t == t1 - P),
                    is_transpose=True,
                )

        def add_up(h, count, t0, t1, turned, through, back):
            opened = t0 == 2 * BANK
            addends = [terms[h, r] for r in range(count)]
            if not opened:
                addends.insert(count - 1, ys[h])
            for a, addend in enumerate(addends):
                turn(addend, t0, t1, turned, a == 0 and not opened, a == len(addends) - 1)
            nc.scalar.copy(through[:, 0 : t1 - t0], turned[:, 0 : t1 - t0])
            for t in range(0, t1 - t0, P):
                nc.tensor.transpose(back[:, t : t + P], through[:, t : t + P], ident[:])

        turned_sb = [keep.tile([P, BANK], F32, name=f"turned_sb{i}") for i in range(4)]
        result = [keep.tile([P, T], F32, name=f"result{h}") for h in range(HALVES)]

        def shared_interleave(dst, t0, t1):
            interleave(dst, both[:, :, 2 * t0 : 2 * t1])

        last = len(GROUPS) - 1
        for g in range(3):
            gather(g, 0)
        for g in range(2):
            gather(g, 1)
        shared_interleave(shared[:, PACK * 32 :], 32, 1024)
        shared_interleave(small[:], 1024, T)
        quantize(small[:], SLOTS + 1024, SLOTS + T)
        for g, (s0, s1) in enumerate(GROUPS):
            for c0 in range(0, s1 - s0, BANK):
                c1 = min(c0 + BANK, s1 - s0)
                room = room_of(g, c0)
                interleave(room, picked(g)[:, :, 2 * c0 : 2 * c1])
                quantize(room, place(s0 + c0), place(s0 + c0) + c1 - c0)
            if g + 2 <= last:
                if g > 0:
                    gather(g + 2, 0)
                gather(g + 2, 1)
            experts = list(range(s0 // C, s1 // C))
            if g < last:
                for h in range(HALVES if g in EARLY else 1):
                    for two in in_twos(experts):
                        routed(next_bank(), h, two)
            if g == 2:
                for h in range(HALVES):
                    shared_expert(next_bank(), h, 2 * BANK, T)
                    turn(ys[h], 2 * BANK, T, banks[6 + h], True, False)
        closing = [next_bank(), next_bank()]
        gelus = [expert(closing[i], 0, E - 1, 0, SLOTS - C + i * P, SLOTS - C + (i + 1) * P, y[0][:, SLOTS - C + i * P : SLOTS - C + (i + 1) * P]) for i in range(2)]
        for gelu in gelus:
            gelu()

        shared_interleave(shared[:, 0 : PACK * 32], 0, 32)
        quantize(shared, SLOTS, SLOTS + 1024)
        load_gate(1, 1, "odd")
        load_gate(1, 2, "grouped")
        spare = [next_bank(), next_bank()]
        for i in range(2):
            shared_expert(spare[i], 0, i * BANK, (i + 1) * BANK)
        deferred = [e for g, (s0, s1) in enumerate(GROUPS) if g not in EARLY for e in range(s0 // C, s1 // C)]
        for i, two in enumerate(in_twos(deferred)):
            routed(closing[i % 2], 1, two)
        for i in range(2):
            shared_expert(closing[i], 1, i * BANK, (i + 1) * BANK)
        for i, (t0, t1) in enumerate(PIECES[0]):
            for r in range(TOP):
                weigh(0, r, t0, t1)
            add_up(0, TOP, t0, t1, banks[4 + i], turned_sb[i % 2], spare[i % 2])
            nc.scalar.copy(result[0][:, t0:t1], spare[i % 2][:, 0 : t1 - t0])
            nc.sync.dma_start(out[0:P, t0:t1], result[0][:, t0:t1])
        held = [closing[0], closing[1], banks[6]]
        for i, (t0, t1) in enumerate(PIECES[0]):
            for r in range(TOP - 1):
                weigh(1, r, t0, t1)
            add_up(1, TOP - 1, t0, t1, banks[(4, 5, 7)[i]], turned_sb[2 + i % 2], held[i])
        for t0, t1 in PIECES[1]:
            weigh(1, TOP - 1, t0, t1)
        for t0, t1 in PIECES[1]:
            at = t0 % BANK
            nc.vector.tensor_tensor(result[1][:, t0:t1], held[t0 // BANK][:, at : at + t1 - t0], terms[1, TOP - 1][:, t0:t1], ADD)
            nc.sync.dma_start(out[P : 2 * P, t0:t1], result[1][:, t0:t1])
